import numpy as np
import ml_dtypes


def mxq(x, axis, fmt="e4m3"):
    dtype, down = {"e4m3": (ml_dtypes.float8_e4m3fn, 7), "e5m2": (ml_dtypes.float8_e5m2, 14)}[fmt]
    v = np.moveaxis(np.asarray(x, np.float32).astype(ml_dtypes.bfloat16).astype(np.float64), axis, -1)
    blocks = v.reshape(v.shape[:-1] + (-1, 32))
    amax = np.abs(blocks).max(-1, keepdims=True)
    byte = np.maximum(np.where(amax > 0, np.frexp(amax)[1] - 1 + 127, 0) - down, 1)
    scale = np.exp2(byte - 127.0)
    codes = (blocks / scale).astype(np.float32).astype(dtype).astype(np.float64)
    return np.moveaxis((codes * scale).reshape(v.shape), -1, axis)


WIDE = False


def mx_kscale(k):
    if not WIDE:
        return np.ones(k)
    levels = np.array([10, -10, 5, -5, 0])
    if k % 512:
        return np.exp2(np.random.permutation(np.resize(levels, k // 32))).repeat(32)
    a = np.empty((k // 512, 16))
    for p in range(k // 512):
        a[p, :8] = np.random.permutation(np.resize(levels, 8))
        for g in range(8):
            far = levels[np.abs(levels - a[p, g]) >= 10]
            a[p, g + 8] = far[np.random.randint(len(far))]
    return np.exp2(a.ravel()).repeat(32)


def f64(x):
    return np.asarray(x).astype(np.float64)


def striped8(idx):
    return np.concatenate([v.reshape(-1, 16).T for v in idx]).astype(np.uint16)


def unstriped8(offs):
    return np.stack([offs[16 * g:16 * g + 16].T.reshape(-1) for g in range(8)]).astype(np.int64)


E2M1 = np.array([0.0, 0.5, 1.0, 1.5, 2.0, 3.0, 4.0, 6.0, -0.0, -0.5, -1.0, -1.5, -2.0, -3.0, -4.0, -6.0])


def pack_weight(w, fmt):
    k, n = w.shape
    w = f64(np.asarray(w, np.float32).astype(ml_dtypes.bfloat16)).reshape(k // 32, 32, n)
    amax = np.abs(w).max(1)
    if fmt == "e4m3":
        byte = np.frexp(amax)[1] - 1 + 127 - 7
    else:
        mant, ex = np.frexp(amax / 6.0)
        byte = np.where(mant > 0.5, ex, ex - 1) + 127
    byte = np.clip(np.where(amax > 0, byte, 1), 1, 254)
    scaled = (w * np.exp2(127.0 - byte)[:, None, :]).reshape(k, n).astype(np.float32)
    by_word = np.ascontiguousarray(scaled.reshape(k // 512, 128, 4, n).transpose(0, 1, 3, 2))
    if fmt == "e4m3":
        words = by_word.astype(ml_dtypes.float8_e4m3fn).view(np.uint8)
    else:
        c = by_word.astype(ml_dtypes.float4_e2m1fn).view(np.uint8) & 0xF
        words = (c[..., 0::2] | (c[..., 1::2] << 4)).reshape(k // 512, 128, 2 * n)
    return np.ascontiguousarray(words), np.ascontiguousarray(byte.astype(np.uint8).reshape(k // 512, 16, n))


def unpack_weight(words, scales, fmt):
    g, _, n = scales.shape
    words = np.ascontiguousarray(words).reshape(g, 128, n, -1)
    if fmt == "e4m3":
        vals = words.view(ml_dtypes.float8_e4m3fn).astype(np.float64)
    else:
        nib = np.empty((g, 128, n, 4), np.uint8)
        nib[..., 0::2] = words & 0xF
        nib[..., 1::2] = words >> 4
        vals = E2M1[nib]
    vals = vals * np.repeat(np.exp2(scales.astype(np.float64) - 127.0), 8, axis=1)[..., None]
    return vals.transpose(0, 1, 3, 2).reshape(g * 512, n)


K, M, T, S = 1024, 256, 1024, 512


def setup_inputs():
    n = np.random.standard_normal
    s = mx_kscale(K)[:, None]
    p_w = pack_weight(n((K, M)) / np.sqrt(K) / s, "e2m1")
    return {
        "xT": (n((K, T)) * s).astype(np.float32),
        "w_words": p_w[0],
        "w_scales": p_w[1],
        "wgt": np.repeat(np.random.uniform(0.5, 2.0, (8, S)), 16, axis=0).astype(np.float32),
        "offs": striped8(np.stack([np.random.permutation(T)[:S] for _ in range(8)])),
    }


def reference(xT, w_words, w_scales, wgt, offs):
    idx = unstriped8(offs)
    group = np.arange(K) % 512 // 64
    xg = f64(wgt)[np.arange(K) // 4 % 128] * f64(xT)[np.arange(K)[:, None], idx[group]]
    xT_ = mxq(xg, 0, "e4m3")
    w_ = unpack_weight(w_words, w_scales, "e2m1")
    y = xT_.T @ w_
    return y

@@ -1,0 +1,137 @@
+from contextlib import ExitStack
+
+import concourse.mybir as mybir
+
+K, N_OUT, T, S = 1024, 256, 1024, 512
+FLOPS = 2 * K * N_OUT * S
+
+F32 = mybir.dt.float32
+BF16 = mybir.dt.bfloat16
+I32 = mybir.dt.int32
+U32 = mybir.dt.uint32
+U16 = mybir.dt.uint16
+U8 = mybir.dt.uint8
+E4M3X4 = mybir.dt.float8_e4m3fn_x4
+E2M1X4 = mybir.dt.float4_e2m1fn_x4
+MULT = mybir.AluOpType.mult
+
+P = 128
+PACK = 4
+K_PASS = P * PACK
+PASSES = K // K_PASS
+HALF = 128
+
+
+def tile_list_heads_tm_none_kernel(tc, xT, w_words, w_scales, wgt, offs, out):
+    nc = tc.nc
+    with ExitStack() as ctx:
+        keep = ctx.enter_context(tc.tile_pool(name="keep", bufs=1))
+        psum = ctx.enter_context(tc.psum_pool(name="psum", bufs=1))
+
+        lists = keep.tile([P, S // 16], U16, name="lists")
+        weight = [keep.tile([P, S // 2], F32, name="wgt%d" % h) for h in range(2)]
+        planes = [[keep.tile([P, T], F32, name="x%d%d" % (a, i)) for i in range(PACK)] for a in range(PASSES)]
+        picked = [keep.tile([P, PACK, S], F32, name="picked%d" % a) for a in range(PASSES)]
+        grouped = [keep.tile([P, S, PACK], BF16, name="grouped%d" % a, align_bytes=64) for a in range(PASSES)]
+        codes = [keep.tile([P, S], U32, name="codes%d" % a, align_bytes=64) for a in range(PASSES)]
+        scales = [keep.tile([P, S], U8, name="scales%d" % a, align_bytes=64) for a in range(PASSES)]
+        w_codes = keep.tile([P, PASSES, 2 * N_OUT], U8, name="w_codes", align_bytes=64)
+        w_sc = keep.tile([P, PASSES, N_OUT], U8, name="w_sc", align_bytes=64)
+        results = [keep.tile([P, N_OUT], F32, name="result%d" % m) for m in range(S // P)]
+        banks = [[psum.tile([P, HALF], F32, name="bank%d%d" % (m, h)) for h in range(2)] for m in range(S // P)]
+        warm = keep.tile([P, 2], F32, name="warm")
+
+        x_view = xT.rearrange("(a p i) t -> a p i t", a=PASSES, i=PACK)
+
+        def load_plane(a, i):
+            nc.sync.dma_start(out=planes[a][i][:], in_=x_view[a, :, i, :])
+
+        nc.gpsimd.memset(w_sc[:].bitcast(I32), 0)
+        nc.gpsimd.memset(warm[:], 0.0)
+        nc.scalar.copy(warm[:, 1:2], warm[:, 0:1])
+        nc.sync.dma_start(lists[:], offs)
+        nc.sync.dma_start(out=weight[0][:], in_=wgt[:, 0 : S // 2])
+        load_plane(0, 0)
+        nc.sync.dma_start(out=weight[1][:], in_=wgt[:, S // 2 : S])
+        for i in range(1, PACK):
+            load_plane(0, i)
+        for i in (0, 1):
+            load_plane(1, i)
+        for q in range(4):
+            nc.sync.dma_start(
+                out=w_sc[32 * q : 32 * q + 4, :, :].bitcast(I32),
+                in_=w_scales.bitcast(I32)[:, 4 * q : 4 * q + 4, :].rearrange("a q n -> q a n"),
+            )
+        for i in (2, 3):
+            load_plane(1, i)
+        nc.sync.dma_start(out=w_codes[:].bitcast(I32), in_=w_words.bitcast(I32).rearrange("a p n -> p a n"))
+
+
+        def pick(a, i, c0, c1):
+            h = c0 // (S // 2)
+            nc.vector.tensor_tensor(
+                picked[a][:, i, c0:c1],
+                planes[a][i][:].indirect(lists[:, c0 // 16 : c1 // 16]),
+                weight[h][:, c0 - h * (S // 2) : c1 - h * (S // 2)],
+                MULT,
+            )
+
+        def interleave(copy, a, c0, c1):
+            copy(
+                grouped[a][:, c0:c1, :].rearrange("p (c n) i -> p c i n", n=4),
+                picked[a][:, :, c0:c1].rearrange("p i (c n) -> p c i n", n=4),
+            )
+
+        def quantise(a, c0, c1):
+            nc.vector.quantize_mx(
+                out=codes[a][:, c0:c1].bitcast(E4M3X4),
+                scales=scales[a][:, c0:c1],
+                in_=grouped[a][:, c0:c1, :].rearrange("p n i -> p (n i)"),
+            )
+
+        def multiply(a, m):
+            cols = slice(P * m, P * (m + 1))
+            for h in range(2):
+                nc.tensor.matmul_mx(
+                    out=banks[m][h][:],
+                    lhsT=codes[a][:, cols].bitcast(E4M3X4),
+                    lhsT_scale=scales[a][:, cols],
+                    rhs=w_codes[:, a, 2 * HALF * h : 2 * HALF * (h + 1)].bitcast(E2M1X4),
+                    rhs_scale=w_sc[:, a, HALF * h : HALF * (h + 1)],
+                    start=(a == 0),
+                    stop=(a == PASSES - 1),
+                )
+
+        def finish(m, copies):
+            for h in range(2):
+                copies[h](results[m][:, HALF * h : HALF * (h + 1)], banks[m][h][:])
+            nc.sync.dma_start(out=out[P * m : P * (m + 1), :], in_=results[m][:])
+
+        S_ = nc.scalar.copy
+        V_ = nc.vector.tensor_copy
+
+        halves = ((0, 256), (256, 512))
+        for i in range(PACK):
+            for c0, c1 in halves:
+                pick(0, i, c0, c1)
+        for c0, c1 in halves:
+            interleave(S_, 0, c0, c1)
+        for i in (0, 1):
+            for c0, c1 in halves:
+                pick(1, i, c0, c1)
+        quantise(0, 0, 512)
+        for m in range(4):
+            multiply(0, m)
+        for m in range(4):
+            for i in (2, 3):
+                pick(1, i, 128 * m, 128 * m + 128)
+            if m < 3:
+                interleave(S_, 1, 128 * m, 128 * m + 128)
+            if m > 0:
+                quantise(1, 128 * (m - 1), 128 * m)
+                multiply(1, m - 1)
+                finish(m - 1, (S_, S_))
+        interleave(V_, 1, 384, 512)
+        quantise(1, 384, 512)
+        multiply(1, 3)
+        finish(3, (S_, V_))

@@ -29,7 +29,7 @@ def tile_list_heads_tm_none_kernel(tc, xT, w_words, w_scales, wgt, offs, out):
         psum = ctx.enter_context(tc.psum_pool(name="psum", bufs=1))
 
         lists = keep.tile([P, S // 16], U16, name="lists")
-        weight = [keep.tile([P, S // 2], F32, name="wgt%d" % h) for h in range(2)]
+        weight = [keep.tile([P, n], F32, name="wgt%d" % n) for n in (P, S - P)]
         planes = [[keep.tile([P, T], F32, name="x%d%d" % (a, i)) for i in range(PACK)] for a in range(PASSES)]
         picked = [keep.tile([P, PACK, S], F32, name="picked%d" % a) for a in range(PASSES)]
         grouped = [keep.tile([P, S, PACK], BF16, name="grouped%d" % a, align_bytes=64) for a in range(PASSES)]
@@ -50,29 +50,27 @@ def tile_list_heads_tm_none_kernel(tc, xT, w_words, w_scales, wgt, offs, out):
         nc.gpsimd.memset(warm[:], 0.0)
         nc.scalar.copy(warm[:, 1:2], warm[:, 0:1])
         nc.sync.dma_start(lists[:], offs)
-        nc.sync.dma_start(out=weight[0][:], in_=wgt[:, 0 : S // 2])
+        nc.sync.dma_start(out=weight[0][:], in_=wgt[:, 0:P])
         load_plane(0, 0)
-        nc.sync.dma_start(out=weight[1][:], in_=wgt[:, S // 2 : S])
+        nc.sync.dma_start(out=weight[1][:], in_=wgt[:, P:S])
         for i in range(1, PACK):
             load_plane(0, i)
-        for i in (0, 1):
+        for i in range(PACK):
             load_plane(1, i)
         for q in range(4):
             nc.sync.dma_start(
                 out=w_sc[32 * q : 32 * q + 4, :, :].bitcast(I32),
                 in_=w_scales.bitcast(I32)[:, 4 * q : 4 * q + 4, :].rearrange("a q n -> q a n"),
             )
-        for i in (2, 3):
-            load_plane(1, i)
         nc.sync.dma_start(out=w_codes[:].bitcast(I32), in_=w_words.bitcast(I32).rearrange("a p n -> p a n"))
 
 
         def pick(a, i, c0, c1):
-            h = c0 // (S // 2)
+            h, base = (0, 0) if c0 < P else (1, P)
             nc.vector.tensor_tensor(
                 picked[a][:, i, c0:c1],
                 planes[a][i][:].indirect(lists[:, c0 // 16 : c1 // 16]),
-                weight[h][:, c0 - h * (S // 2) : c1 - h * (S // 2)],
+                weight[h][:, c0 - base : c1 - base],
                 MULT,
             )
 
@@ -111,13 +109,14 @@ def tile_list_heads_tm_none_kernel(tc, xT, w_words, w_scales, wgt, offs, out):
         V_ = nc.vector.tensor_copy
 
         halves = ((0, 256), (256, 512))
+        cuts = ((0, 128), (128, 512))
         for i in range(PACK):
-            for c0, c1 in halves:
+            for c0, c1 in cuts:
                 pick(0, i, c0, c1)
         for c0, c1 in halves:
-            interleave(S_, 0, c0, c1)
+            interleave(nc.scalar.copy, 0, c0, c1)
         for i in (0, 1):
-            for c0, c1 in halves:
+            for c0, c1 in cuts:
                 pick(1, i, c0, c1)
         quantise(0, 0, 512)
         for m in range(4):
@@ -126,12 +125,12 @@ def tile_list_heads_tm_none_kernel(tc, xT, w_words, w_scales, wgt, offs, out):
             for i in (2, 3):
                 pick(1, i, 128 * m, 128 * m + 128)
             if m < 3:
-                interleave(S_, 1, 128 * m, 128 * m + 128)
+                interleave(nc.scalar.copy, 1, 128 * m, 128 * m + 128)
             if m > 0:
                 quantise(1, 128 * (m - 1), 128 * m)
                 multiply(1, m - 1)
                 finish(m - 1, (S_, S_))
-        interleave(V_, 1, 384, 512)
+        interleave(nc.vector.tensor_copy, 1, 384, 512)
         quantise(1, 384, 512)
         multiply(1, 3)
         finish(3, (S_, V_))

from contextlib import ExitStack

import concourse.mybir as mybir

K, N_OUT, T, S = 1024, 256, 1024, 512
FLOPS = 2 * K * N_OUT * S

F32 = mybir.dt.float32
BF16 = mybir.dt.bfloat16
I32 = mybir.dt.int32
U32 = mybir.dt.uint32
U16 = mybir.dt.uint16
U8 = mybir.dt.uint8
E4M3X4 = mybir.dt.float8_e4m3fn_x4
E2M1X4 = mybir.dt.float4_e2m1fn_x4
MULT = mybir.AluOpType.mult

P = 128
PACK = 4
K_PASS = P * PACK
PASSES = K // K_PASS
HALF = 128


def tile_list_heads_tm_none_kernel(tc, xT, w_words, w_scales, wgt, offs, out):
    nc = tc.nc
    with ExitStack() as ctx:
        keep = ctx.enter_context(tc.tile_pool(name="keep", bufs=1))
        psum = ctx.enter_context(tc.psum_pool(name="psum", bufs=1))

        lists = keep.tile([P, S // 16], U16, name="lists")
        weight = [keep.tile([P, n], F32, name="wgt%d" % n) for n in (P, S - P)]
        planes = [[keep.tile([P, T], F32, name="x%d%d" % (a, i)) for i in range(PACK)] for a in range(PASSES)]
        picked = [keep.tile([P, PACK, S], F32, name="picked%d" % a) for a in range(PASSES)]
        grouped = [keep.tile([P, S, PACK], BF16, name="grouped%d" % a, align_bytes=64) for a in range(PASSES)]
        codes = [keep.tile([P, S], U32, name="codes%d" % a, align_bytes=64) for a in range(PASSES)]
        scales = [keep.tile([P, S], U8, name="scales%d" % a, align_bytes=64) for a in range(PASSES)]
        w_codes = keep.tile([P, PASSES, 2 * N_OUT], U8, name="w_codes", align_bytes=64)
        w_sc = keep.tile([P, PASSES, N_OUT], U8, name="w_sc", align_bytes=64)
        results = [keep.tile([P, N_OUT], F32, name="result%d" % m) for m in range(S // P)]
        banks = [[psum.tile([P, HALF], F32, name="bank%d%d" % (m, h)) for h in range(2)] for m in range(S // P)]
        warm = keep.tile([P, 2], F32, name="warm")

        x_view = xT.rearrange("(a p i) t -> a p i t", a=PASSES, i=PACK)

        def load_plane(a, i):
            nc.sync.dma_start(out=planes[a][i][:], in_=x_view[a, :, i, :])

        nc.gpsimd.memset(w_sc[:].bitcast(I32), 0)
        nc.gpsimd.memset(warm[:], 0.0)
        nc.scalar.copy(warm[:, 1:2], warm[:, 0:1])
        nc.sync.dma_start(lists[:], offs)
        nc.sync.dma_start(out=weight[0][:], in_=wgt[:, 0:P])
        load_plane(0, 0)
        nc.sync.dma_start(out=weight[1][:], in_=wgt[:, P:S])
        for i in range(1, PACK):
            load_plane(0, i)
        for i in range(PACK):
            load_plane(1, i)
        for q in range(4):
            nc.sync.dma_start(
                out=w_sc[32 * q : 32 * q + 4, :, :].bitcast(I32),
                in_=w_scales.bitcast(I32)[:, 4 * q : 4 * q + 4, :].rearrange("a q n -> q a n"),
            )
        nc.sync.dma_start(out=w_codes[:].bitcast(I32), in_=w_words.bitcast(I32).rearrange("a p n -> p a n"))


        def pick(a, i, c0, c1):
            h, base = (0, 0) if c0 < P else (1, P)
            nc.vector.tensor_tensor(
                picked[a][:, i, c0:c1],
                planes[a][i][:].indirect(lists[:, c0 // 16 : c1 // 16]),
                weight[h][:, c0 - base : c1 - base],
                MULT,
            )

        def interleave(copy, a, c0, c1):
            copy(
                grouped[a][:, c0:c1, :].rearrange("p (c n) i -> p c i n", n=4),
                picked[a][:, :, c0:c1].rearrange("p i (c n) -> p c i n", n=4),
            )

        def quantise(a, c0, c1):
            nc.vector.quantize_mx(
                out=codes[a][:, c0:c1].bitcast(E4M3X4),
                scales=scales[a][:, c0:c1],
                in_=grouped[a][:, c0:c1, :].rearrange("p n i -> p (n i)"),
            )

        def multiply(a, m):
            cols = slice(P * m, P * (m + 1))
            for h in range(2):
                nc.tensor.matmul_mx(
                    out=banks[m][h][:],
                    lhsT=codes[a][:, cols].bitcast(E4M3X4),
                    lhsT_scale=scales[a][:, cols],
                    rhs=w_codes[:, a, 2 * HALF * h : 2 * HALF * (h + 1)].bitcast(E2M1X4),
                    rhs_scale=w_sc[:, a, HALF * h : HALF * (h + 1)],
                    start=(a == 0),
                    stop=(a == PASSES - 1),
                )

        def finish(m, copies):
            for h in range(2):
                copies[h](results[m][:, HALF * h : HALF * (h + 1)], banks[m][h][:])
            nc.sync.dma_start(out=out[P * m : P * (m + 1), :], in_=results[m][:])

        S_ = nc.scalar.copy
        V_ = nc.vector.tensor_copy

        halves = ((0, 256), (256, 512))
        cuts = ((0, 128), (128, 512))
        for i in range(PACK):
            for c0, c1 in cuts:
                pick(0, i, c0, c1)
        for c0, c1 in halves:
            interleave(nc.scalar.copy, 0, c0, c1)
        for i in (0, 1):
            for c0, c1 in cuts:
                pick(1, i, c0, c1)
        quantise(0, 0, 512)
        for m in range(4):
            multiply(0, m)
        for m in range(4):
            for i in (2, 3):
                pick(1, i, 128 * m, 128 * m + 128)
            if m < 3:
                interleave(nc.scalar.copy, 1, 128 * m, 128 * m + 128)
            if m > 0:
                quantise(1, 128 * (m - 1), 128 * m)
                multiply(1, m - 1)
                finish(m - 1, (S_, S_))
        interleave(nc.vector.tensor_copy, 1, 384, 512)
        quantise(1, 384, 512)
        multiply(1, 3)
        finish(3, (S_, V_))
